import numpy as np
import ml_dtypes


def mxq(x, axis, fmt="e4m3"):
    dtype, down = {"e4m3": (ml_dtypes.float8_e4m3fn, 7), "e5m2": (ml_dtypes.float8_e5m2, 14)}[fmt]
    v = np.moveaxis(np.asarray(x, np.float32).astype(ml_dtypes.bfloat16).astype(np.float64), axis, -1)
    blocks = v.reshape(v.shape[:-1] + (-1, 32))
    amax = np.abs(blocks).max(-1, keepdims=True)
    byte = np.maximum(np.where(amax > 0, np.frexp(amax)[1] - 1 + 127, 0) - down, 1)
    scale = np.exp2(byte - 127.0)
    codes = (blocks / scale).astype(np.float32).astype(dtype).astype(np.float64)
    return np.moveaxis((codes * scale).reshape(v.shape), -1, axis)


WIDE = False


def mx_kscale(k):
    if not WIDE:
        return np.ones(k)
    levels = np.array([10, -10, 5, -5, 0])
    if k % 512:
        return np.exp2(np.random.permutation(np.resize(levels, k // 32))).repeat(32)
    a = np.empty((k // 512, 16))
    for p in range(k // 512):
        a[p, :8] = np.random.permutation(np.resize(levels, 8))
        for g in range(8):
            far = levels[np.abs(levels - a[p, g]) >= 10]
            a[p, g + 8] = far[np.random.randint(len(far))]
    return np.exp2(a.ravel()).repeat(32)


def f64(x):
    return np.asarray(x).astype(np.float64)


def striped(idx):
    return np.tile(idx.reshape(-1, 16).T, (8, 1)).astype(np.uint16)


def unstriped(offs):
    return offs[:16].T.reshape(-1).astype(np.int64)


def striped8(idx):
    return np.concatenate([x.reshape(-1, 16).T for x in idx]).astype(np.uint16)


def runs(offs, k):
    lists = np.stack([offs[16 * r : 16 * r + 16].T.reshape(-1) for r in range(8)]).astype(np.int64)
    return lists[np.arange(k) % 512 // 64]


def pack_weight(w):
    k, n = w.shape
    w = f64(np.asarray(w, np.float32).astype(ml_dtypes.bfloat16)).reshape(k // 32, 32, n)
    amax = np.abs(w).max(1)
    byte = np.clip(np.where(amax > 0, np.frexp(amax)[1] - 1 + 127 - 7, 1), 1, 254)
    scaled = (w * np.exp2(127.0 - byte)[:, None, :]).reshape(k, n).astype(np.float32)
    words = np.ascontiguousarray(scaled.reshape(k // 512, 128, 4, n).transpose(0, 1, 3, 2)).astype(ml_dtypes.float8_e4m3fn).view(np.uint8)
    return words, np.ascontiguousarray(byte.astype(np.uint8).reshape(k // 512, 16, n))


def unpack_weight(words, scales):
    g, p, n, _ = words.shape
    vals = np.ascontiguousarray(words).view(ml_dtypes.float8_e4m3fn).astype(np.float64) * np.repeat(np.exp2(scales.astype(np.float64) - 127.0), 8, axis=1)[..., None]
    return vals.transpose(0, 1, 3, 2).reshape(g * 512, n)


E2M1 = np.array([0.0, 0.5, 1.0, 1.5, 2.0, 3.0, 4.0, 6.0, -0.0, -0.5, -1.0, -1.5, -2.0, -3.0, -4.0, -6.0])


def pack_fp4(w):
    k, n = w.shape
    w = f64(np.asarray(w, np.float32).astype(ml_dtypes.bfloat16)).reshape(k // 32, 32, n)
    amax = np.abs(w).max(1)
    mant, ex = np.frexp(amax / 6.0)
    byte = np.clip(np.where(amax > 0, np.where(mant > 0.5, ex, ex - 1) + 127, 1), 1, 254)
    scaled = (w * np.exp2(127.0 - byte)[:, None, :]).reshape(k, n).astype(np.float32)
    c = np.ascontiguousarray(scaled.reshape(k // 512, 128, 4, n).transpose(0, 1, 3, 2)).astype(ml_dtypes.float4_e2m1fn).view(np.uint8) & 0xF
    words = (c[..., 0::2] | (c[..., 1::2] << 4)).reshape(k // 512, 128, 2 * n)
    return np.ascontiguousarray(words), np.ascontiguousarray(byte.astype(np.uint8).reshape(k // 512, 16, n))


def unpack_fp4(words, scales):
    g, _, n = scales.shape
    words = np.ascontiguousarray(words).reshape(g, 128, n, 2)
    nib = np.empty((g, 128, n, 4), np.uint8)
    nib[..., 0::2] = words & 0xF
    nib[..., 1::2] = words >> 4
    vals = E2M1[nib] * np.repeat(np.exp2(scales.astype(np.float64) - 127.0), 8, axis=1)[..., None]
    return vals.transpose(0, 1, 3, 2).reshape(g * 512, n)


K, T, S, H, G, W = 512, 1024, 512, 512, 2048, 256


def setup_inputs():
    n = np.random.standard_normal
    s = mx_kscale(K)[:, None]
    packed_xT = pack_weight(n((K, T)) * s)
    packed_w1 = pack_fp4(n((K, H)) / np.sqrt(K) / s)
    packed_dT = pack_weight(n((K, G)) / s)
    perm = np.stack([np.random.permutation(S) for _ in range(8)])
    return {
        "x_words": packed_xT[0],
        "x_scales": packed_xT[1],
        "w1_words": packed_w1[0],
        "w1_scales": packed_w1[1],
        "gs": (np.random.uniform(0.5, 1.5, (K, 1)) * s).astype(np.float32),
        "d_words": packed_dT[0],
        "d_scales": packed_dT[1],
        "offs": striped(np.random.permutation(T)[:S]),
        "k1": striped8(np.random.randint(0, G, (8, H))),
        "k2": striped8(np.random.randint(0, G, (8, H))),
        "two": striped(np.random.permutation(T)[:S]),
        "n1": striped8(perm[:, :W]),
        "n2": striped8(perm[:, W:]),
        "n3": striped8(np.stack([np.random.permutation(S) for _ in range(8)])),
    }


def reference(x_words, x_scales, w1_words, w1_scales, gs, d_words, d_scales, offs, k1, k2, two, n1, n2, n3):
    d_k1 = unpack_weight(d_words, d_scales)[np.arange(K)[:, None], runs(k1, K)]
    xq = unpack_weight(x_words, x_scales)[:, unstriped(offs)]
    y = unpack_fp4(w1_words, w1_scales).T @ xq
    z = f64(gs) * y
    d_k2 = unpack_weight(d_words, d_scales)[np.arange(K)[:, None], runs(k2, K)]
    x_two = unpack_weight(x_words, x_scales)[:, unstriped(two)]
    h = 0.0625 * ((d_k1.T @ mxq(z, 0, "e4m3") + d_k2.T @ x_two))
    pa = h[np.arange(H)[:, None], runs(n1, H)]
    pb = h[np.arange(H)[:, None], runs(n2, H)]
    rb = pa - pb
    ra = pa + pb
    ds = np.zeros((H, S))
    ds[np.arange(H)[:, None], runs(n1, H)] = ra
    dt = ds.copy()
    dt[np.arange(H)[:, None], runs(n2, H)] = rb
    return np.maximum(dt, dt[np.arange(H)[:, None], runs(n3, H)])

@@ -1,0 +1,200 @@
+from contextlib import ExitStack
+
+import concourse.mybir as mybir
+
+F32 = mybir.dt.float32
+BF16 = mybir.dt.bfloat16
+I32 = mybir.dt.int32
+U32 = mybir.dt.uint32
+U16 = mybir.dt.uint16
+U8 = mybir.dt.uint8
+FP8X4 = mybir.dt.float8_e4m3fn_x4
+FP4X4 = mybir.dt.float4_e2m1fn_x4
+COPY = mybir.ActivationFunctionType.Copy
+ADD = mybir.AluOpType.add
+MAX = mybir.AluOpType.max
+
+P = 128
+K, T, S, H, G, W = 512, 1024, 512, 512, 2048, 256
+TILES = H // P
+FLOPS = 3 * 2 * K * H * S
+ODD = 14
+
+
+def tile_picked_cmixihaarh_none_p_kernel(
+    tc, x_words, x_scales, w1_words, w1_scales, gs, d_words, d_scales, offs, k1, k2, two, n1, n2, n3, out
+):
+    nc = tc.nc
+    with ExitStack() as ctx:
+        keep = ctx.enter_context(tc.tile_pool(name="keep", bufs=1))
+        psum = ctx.enter_context(tc.psum_pool(name="psum", bufs=1))
+
+        def held(name, cols, dtype):
+            return keep.tile([P, cols], dtype, name=name, align_bytes=64)
+
+        def load_list(name, src):
+            tile = keep.tile([P, src.shape[1]], U16, name=name)
+            nc.sync.dma_start(tile[:], src)
+            return tile
+
+        def load_scale_rows(queue, tile, src, first):
+            for q in range(4):
+                queue.dma_start(
+                    tile[32 * q + first : 32 * q + first + 4, :].bitcast(I32), src[0, 4 * q : 4 * q + 4, :].bitcast(I32)
+                )
+
+        x_tab = held("x_tab", T, U32)
+        x_tab_s = held("x_tab_s", T, U8)
+        d_tab = held("d_tab", G, U32)
+        d_tab_s = held("d_tab_s", G, U8)
+        w_raw = held("w_raw", 2 * H, U8)
+        w_raw_s = held("w_raw_s", H, U8)
+        d_s = held("d_s", 2 * H, U8)
+        nc.vector.memset(w_raw_s[:].bitcast(I32), 0)
+        nc.vector.memset(d_tab_s[:].bitcast(I32), 0)
+        nc.vector.memset(d_s[:].bitcast(I32), 0)
+
+        offs_l = load_list("offs_l", offs)
+        for q in range(4):
+            rows = x_scales[0, 4 * q : 4 * q + 4, :].bitcast(I32)
+            nc.sync.dma_start(x_tab_s[32 * q : 32 * q + 32, :].bitcast(I32), rows.unsqueeze(0).to_broadcast([8, 4, T // 4]))
+        nc.sync.dma_start(x_tab[:].bitcast(I32), x_words[0].rearrange("p n r -> p (n r)").bitcast(I32))
+        nc.sync.dma_start(w_raw[:].bitcast(I32), w1_words[0].bitcast(I32))
+        two_l = load_list("two_l", two)
+        load_scale_rows(nc.sync, w_raw_s, w1_scales, 0)
+        gs_t = held("gs_t", 4, F32)
+        nc.gpsimd.dma_start(gs_t[:], gs.rearrange("(p t) o -> p (t o)", t=4))
+        load_scale_rows(nc.sync, d_tab_s, d_scales, ODD)
+        k1_l = load_list("k1_l", k1)
+        k2_l = load_list("k2_l", k2)
+        nc.sync.dma_start(d_tab[:].bitcast(I32), d_words[0].rearrange("p n r -> p (n r)").bitcast(I32))
+        n1_l = load_list("n1_l", n1)
+        n2_l = load_list("n2_l", n2)
+        n3_l = load_list("n3_l", n3)
+
+        xa = held("xa", S, U32)
+        xa_s = held("xa_s", S, U8)
+        nc.vector.tensor_copy(xa_s[:], x_tab_s[:].indirect(offs_l[:]))
+        nc.vector.tensor_copy(xa[:], x_tab[:].indirect(offs_l[:]))
+        w = held("w", 2 * H, U8)
+        w_s = held("w_s", H, U8)
+        nc.scalar.copy(
+            w[:].bitcast(U16).rearrange("p (t m) -> p t m", t=4), w_raw[:].bitcast(U16).rearrange("p (m t) -> p t m", t=4)
+        )
+        nc.gpsimd.tensor_copy(w_s[:].rearrange("p (t m) -> p t m", t=4), w_raw_s[:].rearrange("p (m t) -> p t m", t=4))
+        z_planes = held("z_planes", 4 * S, BF16)
+        for t in range(4):
+            y = psum.tile([P, S], F32, name="y%d" % t)
+            nc.tensor.matmul_mx(
+                out=y[:],
+                lhsT=w[:, 2 * P * t : 2 * P * (t + 1)].bitcast(FP4X4),
+                lhsT_scale=w_s[:, P * t : P * (t + 1)],
+                rhs=xa[:].bitcast(FP8X4),
+                rhs_scale=xa_s[:],
+                start=True,
+                stop=True,
+            )
+            nc.scalar.activation(z_planes[:, S * t : S * (t + 1)], y[:], COPY, scale=gs_t[:, t : t + 1])
+        z_bf = held("z_bf", 4 * S, BF16)
+        nc.scalar.copy(
+            z_bf[:].rearrange("p (c i t) -> p c t i", i=4, t=4), z_planes[:].rearrange("p (t c i) -> p c t i", t=4, i=4)
+        )
+
+        xb = held("xb", S, U32)
+        xb_s = held("xb_s", S, U8)
+        nc.vector.tensor_copy(xb_s[:], x_tab_s[:].indirect(two_l[:]))
+
+        picked_s = held("picked_s", 2 * H, U8)
+        nc.vector.tensor_copy(picked_s[:, 0:H], d_tab_s[:].indirect(k1_l[:]))
+        nc.vector.tensor_copy(picked_s[:, H : 2 * H], d_tab_s[:].indirect(k2_l[:]))
+        dealt_s = held("dealt_s", 2 * H, U8)
+        nc.vector.tensor_copy(
+            dealt_s[:].bitcast(I32).rearrange("p (u t r c) -> p u t r c", u=2, t=4, r=8),
+            picked_s[:].bitcast(I32).rearrange("p (u r t c) -> p u t r c", u=2, t=4, r=8),
+        )
+        for q in range(4):
+            nc.sync.dma_start(
+                d_s[32 * q : 32 * q + 4, :].bitcast(I32), dealt_s[32 * q + ODD : 32 * q + ODD + 4, :].bitcast(I32)
+            )
+
+        nc.vector.tensor_copy(xb[:], x_tab[:].indirect(two_l[:]))
+        picked1 = held("picked1", H, U32)
+        picked2 = held("picked2", H, U32)
+        nc.vector.tensor_copy(picked2[:], d_tab[:].indirect(k2_l[:]))
+        nc.vector.tensor_copy(picked1[:], d_tab[:].indirect(k1_l[:]))
+
+        def deal(name, picked, lo, hi):
+            dealt = held(name, P * (hi - lo), U32)
+            nc.vector.tensor_copy(
+                dealt[:].rearrange("p (t r c) -> p t r c", r=8, c=16),
+                picked[:].rearrange("p (r t c) -> p t r c", t=4, r=8)[:, lo:hi],
+            )
+            return [dealt[:, P * i : P * (i + 1)] for i in range(hi - lo)]
+
+        d2 = deal("d2_first", picked2, 0, 1)
+        d1 = deal("d1_first", picked1, 0, 1)
+        z = held("z", S, U32)
+        z_s = held("z_s", S, U8)
+        nc.vector.quantize_mx(out=z[:].bitcast(FP8X4), scales=z_s[:], in_=z_bf[:])
+        d2 = d2 + deal("d2_rest", picked2, 1, TILES)
+        d1 = d1 + deal("d1_rest", picked1, 1, TILES)
+
+        banks = [psum.tile([P, S], F32, name="hsum%d" % t) for t in range(TILES)]
+        for t in range(TILES):
+            nc.tensor.matmul_mx(
+                out=banks[t][:],
+                lhsT=d2[t].bitcast(FP8X4),
+                lhsT_scale=d_s[:, H + P * t : H + P * (t + 1)],
+                rhs=xb[:].bitcast(FP8X4),
+                rhs_scale=xb_s[:],
+                start=True,
+                stop=False,
+            )
+            nc.tensor.matmul_mx(
+                out=banks[t][:],
+                lhsT=d1[t].bitcast(FP8X4),
+                lhsT_scale=d_s[:, P * t : P * (t + 1)],
+                rhs=z[:].bitcast(FP8X4),
+                rhs_scale=z_s[:],
+                start=False,
+                stop=True,
+            )
+
+        out_rows = out.rearrange("(r t c) n -> t r c n", r=8, t=4)
+        dts = []
+
+        def pair_up(t):
+            h = keep.tile([P, S], F32, name="h", tag="rows")
+            nc.scalar.activation(h[:], banks[t][:], COPY, scale=0.0625)
+            pa = held("pa%d" % t, W, F32)
+            pb = held("pb%d" % t, W, F32)
+            nb = held("nb%d" % t, W, F32)
+            nc.scalar.activation(pb[:], h[:].indirect(n2_l[:]), COPY)
+            if t == 0:
+                nc.vector.tensor_copy(pa[:], h[:].indirect(n1_l[:]))
+            else:
+                nc.scalar.activation(pa[:], h[:].indirect(n1_l[:]), COPY)
+            nc.scalar.activation(nb[:], pb[:], COPY, scale=-1.0)
+            dt = held("dt%d" % t, S, F32)
+            nc.vector.tensor_tensor(dt[:].indirect(n1_l[:]), pa[:], pb[:], ADD)
+            nc.vector.tensor_tensor(dt[:].indirect(n2_l[:]), pa[:], nb[:], ADD)
+            dts.append(dt)
+
+        def finish(t, other):
+            dt = dts[t]
+            res = held("res%d" % t, S, F32)
+            for u in range(2):
+                cols = slice(W * u, W * (u + 1))
+                nc.scalar.activation(other[:, cols], dt[:].indirect(n3_l[:, 16 * u : 16 * (u + 1)]), COPY)
+                if t == TILES - 1:
+                    nc.vector.tensor_tensor(res[:, cols], dt[:, cols], other[:, cols], MAX)
+                    nc.sync.dma_start(out_rows[t][:, :, cols], res[:, cols])
+            if t < TILES - 1:
+                nc.vector.tensor_tensor(res[:], dt[:], other[:], MAX)
+                nc.sync.dma_start(out_rows[t], res[:])
+
+        for t in range(TILES):
+            pair_up(t)
+        others = keep.tile([P, TILES, S], F32, name="others", tag="rows")
+        for t in range(TILES):
+            finish(t, others[:, t, :])

@@ -29,8 +29,8 @@ def tile_picked_cmixihaarh_none_p_kernel(
         keep = ctx.enter_context(tc.tile_pool(name="keep", bufs=1))
         psum = ctx.enter_context(tc.psum_pool(name="psum", bufs=1))
 
-        def held(name, cols, dtype):
-            return keep.tile([P, cols], dtype, name=name, align_bytes=64)
+        def held(name, cols, dtype, tag=""):
+            return keep.tile([P, cols], dtype, name=name, align_bytes=64, tag=tag)
 
         def load_list(name, src):
             tile = keep.tile([P, src.shape[1]], U16, name=name)
@@ -45,23 +45,27 @@ def tile_picked_cmixihaarh_none_p_kernel(
 
         x_tab = held("x_tab", T, U32)
         x_tab_s = held("x_tab_s", T, U8)
-        d_tab = held("d_tab", G, U32)
+        d_tab = held("d_tab", G, U32, tag="dict")
         d_tab_s = held("d_tab_s", G, U8)
         w_raw = held("w_raw", 2 * H, U8)
         w_raw_s = held("w_raw_s", H, U8)
         d_s = held("d_s", 2 * H, U8)
-        nc.vector.memset(w_raw_s[:].bitcast(I32), 0)
         nc.vector.memset(d_tab_s[:].bitcast(I32), 0)
         nc.vector.memset(d_s[:].bitcast(I32), 0)
 
+        def load_repeated(tile, src):
+            for q in range(4):
+                rows = src[0, 4 * q : 4 * q + 4, :].bitcast(I32)
+                nc.sync.dma_start(
+                    tile[32 * q : 32 * q + 32, :].bitcast(I32), rows.unsqueeze(0).to_broadcast([8, 4, src.shape[2] // 4])
+                )
+
         offs_l = load_list("offs_l", offs)
-        for q in range(4):
-            rows = x_scales[0, 4 * q : 4 * q + 4, :].bitcast(I32)
-            nc.sync.dma_start(x_tab_s[32 * q : 32 * q + 32, :].bitcast(I32), rows.unsqueeze(0).to_broadcast([8, 4, T // 4]))
+        load_repeated(x_tab_s, x_scales)
         nc.sync.dma_start(x_tab[:].bitcast(I32), x_words[0].rearrange("p n r -> p (n r)").bitcast(I32))
+        load_repeated(w_raw_s, w1_scales)
         nc.sync.dma_start(w_raw[:].bitcast(I32), w1_words[0].bitcast(I32))
         two_l = load_list("two_l", two)
-        load_scale_rows(nc.sync, w_raw_s, w1_scales, 0)
         gs_t = held("gs_t", 4, F32)
         nc.gpsimd.dma_start(gs_t[:], gs.rearrange("(p t) o -> p (t o)", t=4))
         load_scale_rows(nc.sync, d_tab_s, d_scales, ODD)
@@ -81,7 +85,7 @@ def tile_picked_cmixihaarh_none_p_kernel(
         nc.scalar.copy(
             w[:].bitcast(U16).rearrange("p (t m) -> p t m", t=4), w_raw[:].bitcast(U16).rearrange("p (m t) -> p t m", t=4)
         )
-        nc.gpsimd.tensor_copy(w_s[:].rearrange("p (t m) -> p t m", t=4), w_raw_s[:].rearrange("p (m t) -> p t m", t=4))
+        nc.vector.tensor_copy(w_s[:].rearrange("p (t m) -> p t m", t=4), w_raw_s[:].rearrange("p (m t) -> p t m", t=4))
         z_planes = held("z_planes", 4 * S, BF16)
         for t in range(4):
             y = psum.tile([P, S], F32, name="y%d" % t)
@@ -100,23 +104,23 @@ def tile_picked_cmixihaarh_none_p_kernel(
             z_bf[:].rearrange("p (c i t) -> p c t i", i=4, t=4), z_planes[:].rearrange("p (t c i) -> p c t i", t=4, i=4)
         )
 
-        xb = held("xb", S, U32)
         xb_s = held("xb_s", S, U8)
         nc.vector.tensor_copy(xb_s[:], x_tab_s[:].indirect(two_l[:]))
 
-        picked_s = held("picked_s", 2 * H, U8)
+        picked_s = held("picked_s", 2 * H, U8, tag="second")
         nc.vector.tensor_copy(picked_s[:, 0:H], d_tab_s[:].indirect(k1_l[:]))
         nc.vector.tensor_copy(picked_s[:, H : 2 * H], d_tab_s[:].indirect(k2_l[:]))
         dealt_s = held("dealt_s", 2 * H, U8)
         nc.vector.tensor_copy(
-            dealt_s[:].bitcast(I32).rearrange("p (u t r c) -> p u t r c", u=2, t=4, r=8),
-            picked_s[:].bitcast(I32).rearrange("p (u r t c) -> p u t r c", u=2, t=4, r=8),
+            dealt_s[:].bitcast(I32).rearrange("p (u t a b) -> p u t a b", u=2, t=4, a=16),
+            picked_s[:].bitcast(I32).rearrange("p (u a t b) -> p u t a b", u=2, t=4, a=16),
         )
         for q in range(4):
             nc.sync.dma_start(
                 d_s[32 * q : 32 * q + 4, :].bitcast(I32), dealt_s[32 * q + ODD : 32 * q + ODD + 4, :].bitcast(I32)
             )
 
+        xb = held("xb", S, U32, tag="second")
         nc.vector.tensor_copy(xb[:], x_tab[:].indirect(two_l[:]))
         picked1 = held("picked1", H, U32)
         picked2 = held("picked2", H, U32)
@@ -126,14 +130,14 @@ def tile_picked_cmixihaarh_none_p_kernel(
         def deal(name, picked, lo, hi):
             dealt = held(name, P * (hi - lo), U32)
             nc.vector.tensor_copy(
-                dealt[:].rearrange("p (t r c) -> p t r c", r=8, c=16),
-                picked[:].rearrange("p (r t c) -> p t r c", t=4, r=8)[:, lo:hi],
+                dealt[:].bitcast(I32).rearrange("p (t a b) -> p a t b", a=16, b=8),
+                picked[:].bitcast(I32).rearrange("p (a t b) -> p a t b", t=4, a=16)[:, :, lo:hi],
             )
             return [dealt[:, P * i : P * (i + 1)] for i in range(hi - lo)]
 
         d2 = deal("d2_first", picked2, 0, 1)
         d1 = deal("d1_first", picked1, 0, 1)
-        z = held("z", S, U32)
+        z = held("z", S, U32, tag="dict")
         z_s = held("z_s", S, U8)
         nc.vector.quantize_mx(out=z[:].bitcast(FP8X4), scales=z_s[:], in_=z_bf[:])
         d2 = d2 + deal("d2_rest", picked2, 1, TILES)
@@ -160,7 +164,7 @@ def tile_picked_cmixihaarh_none_p_kernel(
                 stop=True,
             )
 
-        out_rows = out.rearrange("(r t c) n -> t r c n", r=8, t=4)
+        out_rows = out.rearrange("(a t b) n -> t a b n", a=16, t=4)
         dts = []
 
         def pair_up(t):

@@ -63,14 +63,14 @@ def tile_picked_cmixihaarh_none_p_kernel(
         offs_l = load_list("offs_l", offs)
         load_repeated(x_tab_s, x_scales)
         nc.sync.dma_start(x_tab[:].bitcast(I32), x_words[0].rearrange("p n r -> p (n r)").bitcast(I32))
-        load_repeated(w_raw_s, w1_scales)
         nc.sync.dma_start(w_raw[:].bitcast(I32), w1_words[0].bitcast(I32))
-        two_l = load_list("two_l", two)
+        load_repeated(w_raw_s, w1_scales)
         gs_t = held("gs_t", 4, F32)
         nc.gpsimd.dma_start(gs_t[:], gs.rearrange("(p t) o -> p (t o)", t=4))
         load_scale_rows(nc.sync, d_tab_s, d_scales, ODD)
         k1_l = load_list("k1_l", k1)
         k2_l = load_list("k2_l", k2)
+        two_l = load_list("two_l", two)
         nc.sync.dma_start(d_tab[:].bitcast(I32), d_words[0].rearrange("p n r -> p (n r)").bitcast(I32))
         n1_l = load_list("n1_l", n1)
         n2_l = load_list("n2_l", n2)
@@ -88,7 +88,7 @@ def tile_picked_cmixihaarh_none_p_kernel(
         nc.vector.tensor_copy(w_s[:].rearrange("p (t m) -> p t m", t=4), w_raw_s[:].rearrange("p (m t) -> p t m", t=4))
         z_planes = held("z_planes", 4 * S, BF16)
         for t in range(4):
-            y = psum.tile([P, S], F32, name="y%d" % t)
+            y = psum.tile([P, S], F32, name="y", tag="y%d" % t)
             nc.tensor.matmul_mx(
                 out=y[:],
                 lhsT=w[:, 2 * P * t : 2 * P * (t + 1)].bitcast(FP4X4),
@@ -105,11 +105,11 @@ def tile_picked_cmixihaarh_none_p_kernel(
         )
 
         xb_s = held("xb_s", S, U8)
-        nc.vector.tensor_copy(xb_s[:], x_tab_s[:].indirect(two_l[:]))
 
-        picked_s = held("picked_s", 2 * H, U8, tag="second")
+        picked_s = held("picked_s", 2 * H, U8)
         nc.vector.tensor_copy(picked_s[:, 0:H], d_tab_s[:].indirect(k1_l[:]))
         nc.vector.tensor_copy(picked_s[:, H : 2 * H], d_tab_s[:].indirect(k2_l[:]))
+        nc.vector.tensor_copy(xb_s[:], x_tab_s[:].indirect(two_l[:]))
         dealt_s = held("dealt_s", 2 * H, U8)
         nc.vector.tensor_copy(
             dealt_s[:].bitcast(I32).rearrange("p (u t a b) -> p u t a b", u=2, t=4, a=16),
@@ -120,7 +120,7 @@ def tile_picked_cmixihaarh_none_p_kernel(
                 d_s[32 * q : 32 * q + 4, :].bitcast(I32), dealt_s[32 * q + ODD : 32 * q + ODD + 4, :].bitcast(I32)
             )
 
-        xb = held("xb", S, U32, tag="second")
+        xb = held("xb", S, U32)
         nc.vector.tensor_copy(xb[:], x_tab[:].indirect(two_l[:]))
         picked1 = held("picked1", H, U32)
         picked2 = held("picked2", H, U32)
@@ -139,66 +139,81 @@ def tile_picked_cmixihaarh_none_p_kernel(
         d1 = deal("d1_first", picked1, 0, 1)
         z = held("z", S, U32, tag="dict")
         z_s = held("z_s", S, U8)
-        nc.vector.quantize_mx(out=z[:].bitcast(FP8X4), scales=z_s[:], in_=z_bf[:])
+        for u in range(2):
+            cols = slice(W * u, W * (u + 1))
+            nc.vector.quantize_mx(out=z[:, cols].bitcast(FP8X4), scales=z_s[:, cols], in_=z_bf[:, 4 * W * u : 4 * W * (u + 1)])
         d2 = d2 + deal("d2_rest", picked2, 1, TILES)
         d1 = d1 + deal("d1_rest", picked1, 1, TILES)
 
-        banks = [psum.tile([P, S], F32, name="hsum%d" % t) for t in range(TILES)]
+        sums = []
         for t in range(TILES):
-            nc.tensor.matmul_mx(
-                out=banks[t][:],
-                lhsT=d2[t].bitcast(FP8X4),
-                lhsT_scale=d_s[:, H + P * t : H + P * (t + 1)],
-                rhs=xb[:].bitcast(FP8X4),
-                rhs_scale=xb_s[:],
-                start=True,
-                stop=False,
-            )
-            nc.tensor.matmul_mx(
-                out=banks[t][:],
-                lhsT=d1[t].bitcast(FP8X4),
-                lhsT_scale=d_s[:, P * t : P * (t + 1)],
-                rhs=z[:].bitcast(FP8X4),
-                rhs_scale=z_s[:],
-                start=False,
-                stop=True,
-            )
+            pieces = [slice(0, W), slice(W, S)] if t == 0 else [slice(0, S)]
+            banks = [psum.tile([P, c.stop - c.start], F32, name="hsum", tag="y%d" % ((t + i) % 4) if t == 0 else "h%d" % t) for i, c in enumerate(pieces)]
+            for bank, cols in zip(banks, pieces):
+                nc.tensor.matmul_mx(
+                    out=bank[:],
+                    lhsT=d2[t].bitcast(FP8X4),
+                    lhsT_scale=d_s[:, H + P * t : H + P * (t + 1)],
+                    rhs=xb[:, cols].bitcast(FP8X4),
+                    rhs_scale=xb_s[:, cols],
+                    start=True,
+                    stop=False,
+                )
+            for bank, cols in zip(banks, pieces):
+                nc.tensor.matmul_mx(
+                    out=bank[:],
+                    lhsT=d1[t].bitcast(FP8X4),
+                    lhsT_scale=d_s[:, P * t : P * (t + 1)],
+                    rhs=z[:, cols].bitcast(FP8X4),
+                    rhs_scale=z_s[:, cols],
+                    start=False,
+                    stop=True,
+                )
+            sums.append(list(zip(banks, pieces)))
 
         out_rows = out.rearrange("(a t b) n -> t a b n", a=16, t=4)
-        dts = []
+        pa, pb, dt = [], [], []
 
-        def pair_up(t):
-            h = keep.tile([P, S], F32, name="h", tag="rows")
-            nc.scalar.activation(h[:], banks[t][:], COPY, scale=0.0625)
-            pa = held("pa%d" % t, W, F32)
-            pb = held("pb%d" % t, W, F32)
-            nb = held("nb%d" % t, W, F32)
-            nc.scalar.activation(pb[:], h[:].indirect(n2_l[:]), COPY)
+        def fetch_pairs(t, tag):
+            h = keep.tile([P, S], F32, name="h", tag=tag)
+            for bank, cols in sums[t]:
+                nc.scalar.activation(h[:, cols], bank[:], COPY, scale=0.0625)
+            pa.append(held("pa%d" % t, W, F32))
+            pb.append(held("pb%d" % t, W, F32))
+            dt.append(held("dt%d" % t, S, F32))
+            nc.scalar.activation(pb[t][:], h[:].indirect(n2_l[:]), COPY)
             if t == 0:
-                nc.vector.tensor_copy(pa[:], h[:].indirect(n1_l[:]))
+                nc.vector.tensor_copy(pa[t][:], h[:].indirect(n1_l[:]))
             else:
-                nc.scalar.activation(pa[:], h[:].indirect(n1_l[:]), COPY)
-            nc.scalar.activation(nb[:], pb[:], COPY, scale=-1.0)
-            dt = held("dt%d" % t, S, F32)
-            nc.vector.tensor_tensor(dt[:].indirect(n1_l[:]), pa[:], pb[:], ADD)
-            nc.vector.tensor_tensor(dt[:].indirect(n2_l[:]), pa[:], nb[:], ADD)
-            dts.append(dt)
+                nc.scalar.activation(pa[t][:], h[:].indirect(n1_l[:]), COPY)
+            nc.vector.tensor_tensor(dt[t][:].indirect(n1_l[:]), pa[t][:], pb[t][:], ADD)
+
+        def put_differences(t, minus_pb):
+            nc.scalar.activation(minus_pb, pb[t][:], COPY, scale=-1.0)
+            nc.vector.tensor_tensor(dt[t][:].indirect(n2_l[:]), pa[t][:], minus_pb, ADD)
 
         def finish(t, other):
-            dt = dts[t]
             res = held("res%d" % t, S, F32)
             for u in range(2):
                 cols = slice(W * u, W * (u + 1))
-                nc.scalar.activation(other[:, cols], dt[:].indirect(n3_l[:, 16 * u : 16 * (u + 1)]), COPY)
+                nc.scalar.activation(other[:, cols], dt[t][:].indirect(n3_l[:, 16 * u : 16 * (u + 1)]), COPY)
                 if t == TILES - 1:
-                    nc.vector.tensor_tensor(res[:, cols], dt[:, cols], other[:, cols], MAX)
+                    nc.vector.tensor_tensor(res[:, cols], dt[t][:, cols], other[:, cols], MAX)
                     nc.sync.dma_start(out_rows[t][:, :, cols], res[:, cols])
             if t < TILES - 1:
-                nc.vector.tensor_tensor(res[:], dt[:], other[:], MAX)
+                nc.vector.tensor_tensor(res[:], dt[t][:], other[:], MAX)
                 nc.sync.dma_start(out_rows[t], res[:])
 
-        for t in range(TILES):
-            pair_up(t)
-        others = keep.tile([P, TILES, S], F32, name="others", tag="rows")
-        for t in range(TILES):
-            finish(t, others[:, t, :])
+        fetch_pairs(0, "rows01")
+        put_differences(0, held("minus0", W, F32)[:])
+        fetch_pairs(1, "rows01")
+        fetch_pairs(2, "rows2")
+        minus1 = keep.tile([P, W], F32, name="minus1", tag="rows2")
+        put_differences(1, minus1[:])
+        fetch_pairs(3, "rows3")
+        late = keep.tile([P, 2 * W + TILES * S], F32, name="late", tag="rows3")
+        put_differences(2, late[:, 0:W])
+        finish(0, late[:, 2 * W : 2 * W + S])
+        put_differences(3, late[:, W : 2 * W])
+        for t in range(1, TILES):
+            finish(t, late[:, 2 * W + S * t : 2 * W + S * (t + 1)])

@@ -18,7 +18,7 @@ P = 128
 K, T, S, H, G, W = 512, 1024, 512, 512, 2048, 256
 TILES = H // P
 FLOPS = 3 * 2 * K * H * S
-ODD = 14
+TAPER = [slice(0, 256), slice(256, 384), slice(384, 512)]
 
 
 def tile_picked_cmixihaarh_none_p_kernel(
@@ -67,7 +67,7 @@ def tile_picked_cmixihaarh_none_p_kernel(
         load_repeated(w_raw_s, w1_scales)
         gs_t = held("gs_t", 4, F32)
         nc.gpsimd.dma_start(gs_t[:], gs.rearrange("(p t) o -> p (t o)", t=4))
-        load_scale_rows(nc.sync, d_tab_s, d_scales, ODD)
+        nc.sync.dma_start(d_tab_s[0:P:8, :].bitcast(I32), d_scales[0].bitcast(I32))
         k1_l = load_list("k1_l", k1)
         k2_l = load_list("k2_l", k2)
         two_l = load_list("two_l", two)
@@ -117,7 +117,7 @@ def tile_picked_cmixihaarh_none_p_kernel(
         )
         for q in range(4):
             nc.sync.dma_start(
-                d_s[32 * q : 32 * q + 4, :].bitcast(I32), dealt_s[32 * q + ODD : 32 * q + ODD + 4, :].bitcast(I32)
+                d_s[32 * q : 32 * q + 4, :].bitcast(I32), dealt_s[32 * q : 32 * q + 32 : 8, :].bitcast(I32)
             )
 
         xb = held("xb", S, U32)
@@ -139,15 +139,14 @@ def tile_picked_cmixihaarh_none_p_kernel(
         d1 = deal("d1_first", picked1, 0, 1)
         z = held("z", S, U32, tag="dict")
         z_s = held("z_s", S, U8)
-        for u in range(2):
-            cols = slice(W * u, W * (u + 1))
-            nc.vector.quantize_mx(out=z[:, cols].bitcast(FP8X4), scales=z_s[:, cols], in_=z_bf[:, 4 * W * u : 4 * W * (u + 1)])
+        for cols in TAPER:
+            nc.vector.quantize_mx(out=z[:, cols].bitcast(FP8X4), scales=z_s[:, cols], in_=z_bf[:, 4 * cols.start : 4 * cols.stop])
         d2 = d2 + deal("d2_rest", picked2, 1, TILES)
         d1 = d1 + deal("d1_rest", picked1, 1, TILES)
 
         sums = []
         for t in range(TILES):
-            pieces = [slice(0, W), slice(W, S)] if t == 0 else [slice(0, S)]
+            pieces = TAPER if t == 0 else [slice(0, S)]
             banks = [psum.tile([P, c.stop - c.start], F32, name="hsum", tag="y%d" % ((t + i) % 4) if t == 0 else "h%d" % t) for i, c in enumerate(pieces)]
             for bank, cols in zip(banks, pieces):
                 nc.tensor.matmul_mx(
@@ -194,9 +193,8 @@ def tile_picked_cmixihaarh_none_p_kernel(
 
         def finish(t, other):
             res = held("res%d" % t, S, F32)
-            for u in range(2):
-                cols = slice(W * u, W * (u + 1))
-                nc.scalar.activation(other[:, cols], dt[t][:].indirect(n3_l[:, 16 * u : 16 * (u + 1)]), COPY)
+            for cols in TAPER if t == TILES - 1 else [slice(0, W), slice(W, S)]:
+                nc.scalar.activation(other[:, cols], dt[t][:].indirect(n3_l[:, cols.start // 16 : cols.stop // 16]), COPY)
                 if t == TILES - 1:
                     nc.vector.tensor_tensor(res[:, cols], dt[t][:, cols], other[:, cols], MAX)
                     nc.sync.dma_start(out_rows[t][:, :, cols], res[:, cols])
@@ -213,7 +211,6 @@ def tile_picked_cmixihaarh_none_p_kernel(
         fetch_pairs(3, "rows3")
         late = keep.tile([P, 2 * W + TILES * S], F32, name="late", tag="rows3")
         put_differences(2, late[:, 0:W])
-        finish(0, late[:, 2 * W : 2 * W + S])
         put_differences(3, late[:, W : 2 * W])
-        for t in range(1, TILES):
+        for t in range(TILES):
             finish(t, late[:, 2 * W + S * t : 2 * W + S * (t + 1)])

from contextlib import ExitStack

import concourse.mybir as mybir

F32 = mybir.dt.float32
BF16 = mybir.dt.bfloat16
I32 = mybir.dt.int32
U32 = mybir.dt.uint32
U16 = mybir.dt.uint16
U8 = mybir.dt.uint8
FP8X4 = mybir.dt.float8_e4m3fn_x4
FP4X4 = mybir.dt.float4_e2m1fn_x4
COPY = mybir.ActivationFunctionType.Copy
ADD = mybir.AluOpType.add
MAX = mybir.AluOpType.max

P = 128
K, T, S, H, G, W = 512, 1024, 512, 512, 2048, 256
TILES = H // P
FLOPS = 3 * 2 * K * H * S
TAPER = [slice(0, 256), slice(256, 384), slice(384, 512)]


def tile_picked_cmixihaarh_none_p_kernel(
    tc, x_words, x_scales, w1_words, w1_scales, gs, d_words, d_scales, offs, k1, k2, two, n1, n2, n3, out
):
    nc = tc.nc
    with ExitStack() as ctx:
        keep = ctx.enter_context(tc.tile_pool(name="keep", bufs=1))
        psum = ctx.enter_context(tc.psum_pool(name="psum", bufs=1))

        def held(name, cols, dtype, tag=""):
            return keep.tile([P, cols], dtype, name=name, align_bytes=64, tag=tag)

        def load_list(name, src):
            tile = keep.tile([P, src.shape[1]], U16, name=name)
            nc.sync.dma_start(tile[:], src)
            return tile

        def load_scale_rows(queue, tile, src, first):
            for q in range(4):
                queue.dma_start(
                    tile[32 * q + first : 32 * q + first + 4, :].bitcast(I32), src[0, 4 * q : 4 * q + 4, :].bitcast(I32)
                )

        x_tab = held("x_tab", T, U32)
        x_tab_s = held("x_tab_s", T, U8)
        d_tab = held("d_tab", G, U32, tag="dict")
        d_tab_s = held("d_tab_s", G, U8)
        w_raw = held("w_raw", 2 * H, U8)
        w_raw_s = held("w_raw_s", H, U8)
        d_s = held("d_s", 2 * H, U8)
        nc.vector.memset(d_tab_s[:].bitcast(I32), 0)
        nc.vector.memset(d_s[:].bitcast(I32), 0)

        def load_repeated(tile, src):
            for q in range(4):
                rows = src[0, 4 * q : 4 * q + 4, :].bitcast(I32)
                nc.sync.dma_start(
                    tile[32 * q : 32 * q + 32, :].bitcast(I32), rows.unsqueeze(0).to_broadcast([8, 4, src.shape[2] // 4])
                )

        offs_l = load_list("offs_l", offs)
        load_repeated(x_tab_s, x_scales)
        nc.sync.dma_start(x_tab[:].bitcast(I32), x_words[0].rearrange("p n r -> p (n r)").bitcast(I32))
        nc.sync.dma_start(w_raw[:].bitcast(I32), w1_words[0].bitcast(I32))
        load_repeated(w_raw_s, w1_scales)
        gs_t = held("gs_t", 4, F32)
        nc.gpsimd.dma_start(gs_t[:], gs.rearrange("(p t) o -> p (t o)", t=4))
        nc.sync.dma_start(d_tab_s[0:P:8, :].bitcast(I32), d_scales[0].bitcast(I32))
        k1_l = load_list("k1_l", k1)
        k2_l = load_list("k2_l", k2)
        two_l = load_list("two_l", two)
        nc.sync.dma_start(d_tab[:].bitcast(I32), d_words[0].rearrange("p n r -> p (n r)").bitcast(I32))
        n1_l = load_list("n1_l", n1)
        n2_l = load_list("n2_l", n2)
        n3_l = load_list("n3_l", n3)

        xa = held("xa", S, U32)
        xa_s = held("xa_s", S, U8)
        nc.vector.tensor_copy(xa_s[:], x_tab_s[:].indirect(offs_l[:]))
        nc.vector.tensor_copy(xa[:], x_tab[:].indirect(offs_l[:]))
        w = held("w", 2 * H, U8)
        w_s = held("w_s", H, U8)
        nc.scalar.copy(
            w[:].bitcast(U16).rearrange("p (t m) -> p t m", t=4), w_raw[:].bitcast(U16).rearrange("p (m t) -> p t m", t=4)
        )
        nc.vector.tensor_copy(w_s[:].rearrange("p (t m) -> p t m", t=4), w_raw_s[:].rearrange("p (m t) -> p t m", t=4))
        z_planes = held("z_planes", 4 * S, BF16)
        for t in range(4):
            y = psum.tile([P, S], F32, name="y", tag="y%d" % t)
            nc.tensor.matmul_mx(
                out=y[:],
                lhsT=w[:, 2 * P * t : 2 * P * (t + 1)].bitcast(FP4X4),
                lhsT_scale=w_s[:, P * t : P * (t + 1)],
                rhs=xa[:].bitcast(FP8X4),
                rhs_scale=xa_s[:],
                start=True,
                stop=True,
            )
            nc.scalar.activation(z_planes[:, S * t : S * (t + 1)], y[:], COPY, scale=gs_t[:, t : t + 1])
        z_bf = held("z_bf", 4 * S, BF16)
        nc.scalar.copy(
            z_bf[:].rearrange("p (c i t) -> p c t i", i=4, t=4), z_planes[:].rearrange("p (t c i) -> p c t i", t=4, i=4)
        )

        xb_s = held("xb_s", S, U8)

        picked_s = held("picked_s", 2 * H, U8)
        nc.vector.tensor_copy(picked_s[:, 0:H], d_tab_s[:].indirect(k1_l[:]))
        nc.vector.tensor_copy(picked_s[:, H : 2 * H], d_tab_s[:].indirect(k2_l[:]))
        nc.vector.tensor_copy(xb_s[:], x_tab_s[:].indirect(two_l[:]))
        dealt_s = held("dealt_s", 2 * H, U8)
        nc.vector.tensor_copy(
            dealt_s[:].bitcast(I32).rearrange("p (u t a b) -> p u t a b", u=2, t=4, a=16),
            picked_s[:].bitcast(I32).rearrange("p (u a t b) -> p u t a b", u=2, t=4, a=16),
        )
        for q in range(4):
            nc.sync.dma_start(
                d_s[32 * q : 32 * q + 4, :].bitcast(I32), dealt_s[32 * q : 32 * q + 32 : 8, :].bitcast(I32)
            )

        xb = held("xb", S, U32)
        nc.vector.tensor_copy(xb[:], x_tab[:].indirect(two_l[:]))
        picked1 = held("picked1", H, U32)
        picked2 = held("picked2", H, U32)
        nc.vector.tensor_copy(picked2[:], d_tab[:].indirect(k2_l[:]))
        nc.vector.tensor_copy(picked1[:], d_tab[:].indirect(k1_l[:]))

        def deal(name, picked, lo, hi):
            dealt = held(name, P * (hi - lo), U32)
            nc.vector.tensor_copy(
                dealt[:].bitcast(I32).rearrange("p (t a b) -> p a t b", a=16, b=8),
                picked[:].bitcast(I32).rearrange("p (a t b) -> p a t b", t=4, a=16)[:, :, lo:hi],
            )
            return [dealt[:, P * i : P * (i + 1)] for i in range(hi - lo)]

        d2 = deal("d2_first", picked2, 0, 1)
        d1 = deal("d1_first", picked1, 0, 1)
        z = held("z", S, U32, tag="dict")
        z_s = held("z_s", S, U8)
        for cols in TAPER:
            nc.vector.quantize_mx(out=z[:, cols].bitcast(FP8X4), scales=z_s[:, cols], in_=z_bf[:, 4 * cols.start : 4 * cols.stop])
        d2 = d2 + deal("d2_rest", picked2, 1, TILES)
        d1 = d1 + deal("d1_rest", picked1, 1, TILES)

        sums = []
        for t in range(TILES):
            pieces = TAPER if t == 0 else [slice(0, S)]
            banks = [psum.tile([P, c.stop - c.start], F32, name="hsum", tag="y%d" % ((t + i) % 4) if t == 0 else "h%d" % t) for i, c in enumerate(pieces)]
            for bank, cols in zip(banks, pieces):
                nc.tensor.matmul_mx(
                    out=bank[:],
                    lhsT=d2[t].bitcast(FP8X4),
                    lhsT_scale=d_s[:, H + P * t : H + P * (t + 1)],
                    rhs=xb[:, cols].bitcast(FP8X4),
                    rhs_scale=xb_s[:, cols],
                    start=True,
                    stop=False,
                )
            for bank, cols in zip(banks, pieces):
                nc.tensor.matmul_mx(
                    out=bank[:],
                    lhsT=d1[t].bitcast(FP8X4),
                    lhsT_scale=d_s[:, P * t : P * (t + 1)],
                    rhs=z[:, cols].bitcast(FP8X4),
                    rhs_scale=z_s[:, cols],
                    start=False,
                    stop=True,
                )
            sums.append(list(zip(banks, pieces)))

        out_rows = out.rearrange("(a t b) n -> t a b n", a=16, t=4)
        pa, pb, dt = [], [], []

        def fetch_pairs(t, tag):
            h = keep.tile([P, S], F32, name="h", tag=tag)
            for bank, cols in sums[t]:
                nc.scalar.activation(h[:, cols], bank[:], COPY, scale=0.0625)
            pa.append(held("pa%d" % t, W, F32))
            pb.append(held("pb%d" % t, W, F32))
            dt.append(held("dt%d" % t, S, F32))
            nc.scalar.activation(pb[t][:], h[:].indirect(n2_l[:]), COPY)
            if t == 0:
                nc.vector.tensor_copy(pa[t][:], h[:].indirect(n1_l[:]))
            else:
                nc.scalar.activation(pa[t][:], h[:].indirect(n1_l[:]), COPY)
            nc.vector.tensor_tensor(dt[t][:].indirect(n1_l[:]), pa[t][:], pb[t][:], ADD)

        def put_differences(t, minus_pb):
            nc.scalar.activation(minus_pb, pb[t][:], COPY, scale=-1.0)
            nc.vector.tensor_tensor(dt[t][:].indirect(n2_l[:]), pa[t][:], minus_pb, ADD)

        def finish(t, other):
            res = held("res%d" % t, S, F32)
            for cols in TAPER if t == TILES - 1 else [slice(0, W), slice(W, S)]:
                nc.scalar.activation(other[:, cols], dt[t][:].indirect(n3_l[:, cols.start // 16 : cols.stop // 16]), COPY)
                if t == TILES - 1:
                    nc.vector.tensor_tensor(res[:, cols], dt[t][:, cols], other[:, cols], MAX)
                    nc.sync.dma_start(out_rows[t][:, :, cols], res[:, cols])
            if t < TILES - 1:
                nc.vector.tensor_tensor(res[:], dt[t][:], other[:], MAX)
                nc.sync.dma_start(out_rows[t], res[:])

        fetch_pairs(0, "rows01")
        put_differences(0, held("minus0", W, F32)[:])
        fetch_pairs(1, "rows01")
        fetch_pairs(2, "rows2")
        minus1 = keep.tile([P, W], F32, name="minus1", tag="rows2")
        put_differences(1, minus1[:])
        fetch_pairs(3, "rows3")
        late = keep.tile([P, 2 * W + TILES * S], F32, name="late", tag="rows3")
        put_differences(2, late[:, 0:W])
        put_differences(3, late[:, W : 2 * W])
        for t in range(TILES):
            finish(t, late[:, 2 * W + S * t : 2 * W + S * (t + 1)])
